import numpy as np
import ml_dtypes

BF16 = ml_dtypes.bfloat16


def bf(x):
    return np.asarray(x, np.float32).astype(BF16)


def f32(x):
    return np.asarray(x, np.float32)


def f64(x):
    return np.asarray(x).astype(np.float64)


def striped(idx):
    return np.tile(idx.reshape(-1, 16).T, (8, 1))


def rows(idx, k):
    return np.tile(idx, (k, 1))


def look(tab, idx):
    return np.take_along_axis(f64(tab), rows(idx, len(tab)), axis=1)


K, S, V, N, M = 256, 2048, 2048, 2048, 128


def setup_inputs():
    return {"tab": f32(np.random.standard_normal((2, K, S))), "w": bf(np.random.standard_normal((K, M)) / np.sqrt(K)), "b": f32(0.5 * np.random.standard_normal((M, 1))), "offs": striped(np.random.permutation(S)[:N])}


def reference(tab, w, b, offs):
    idx = offs[:16].T.reshape(-1)
    x = (np.minimum(np.maximum(look(tab[0], idx), -1.25), 1.0)) * (1.0 / (1.0 + np.exp(-look(tab[1], idx))))
    return np.maximum(f64(w).T @ x + f64(b), 0.0)

@@ -1,0 +1,59 @@
+import concourse.mybir as mybir
+
+F32, BF16, U16 = mybir.dt.float32, mybir.dt.bfloat16, mybir.dt.uint16
+OP = mybir.AluOpType
+FUNC = mybir.ActivationFunctionType
+
+P = 128
+R = 256
+S = 2048
+N = 2048
+M = 128
+BLOCKS = R // P
+PIECE = 512
+LOW, HIGH = -1.25, 1.0
+
+FLOPS = 2 * R * M * N
+
+
+def tile_lookup_vg_clipsig_relu_kernel(tc, tab, w, b, offs, out):
+    nc = tc.nc
+    with (
+        tc.tile_pool(name="held", bufs=1) as held,
+        tc.tile_pool(name="work", bufs=4) as work,
+        tc.psum_pool(name="sums", bufs=1) as sums,
+    ):
+        offsets = held.tile([P, N // 16], U16, name="offsets")
+        nc.sync.dma_start(offsets[:], offs)
+
+        values, gates = [], []
+        for k in range(BLOCKS):
+            rows = slice(k * P, (k + 1) * P)
+            value_window = held.tile([P, S], F32, name=f"value_window{k}")
+            gate_window = held.tile([P, S], F32, name=f"gate_window{k}")
+            nc.sync.dma_start(value_window[:], tab[0, rows, :])
+            nc.sync.dma_start(gate_window[:], tab[1, rows, :])
+            values.append(value_window)
+            gates.append(gate_window)
+
+        weights = held.tile([P, BLOCKS, M], BF16, name="weights")
+        nc.gpsimd.dma_start(weights[:], w.rearrange("(k p) m -> p k m", p=P))
+        bias = held.tile([M, 1], F32, name="bias")
+        nc.gpsimd.dma_start(bias[:], b)
+
+        banks = [sums.tile([M, PIECE], F32, name=f"bank{c}") for c in range(N // PIECE)]
+        for k in range(BLOCKS):
+            for c in range(N // PIECE):
+                piece = offsets[:, c * PIECE // 16 : (c + 1) * PIECE // 16]
+                clamped = work.tile([P, PIECE], F32, name="clamped")
+                nc.vector.tensor_scalar(clamped[:], values[k][:].indirect(piece), LOW, HIGH, OP.max, OP.min)
+                gate = work.tile([P, PIECE], F32, name="gate")
+                nc.scalar.activation(gate[:], gates[k][:].indirect(piece), FUNC.Sigmoid)
+                x = work.tile([P, PIECE], BF16, name="x")
+                nc.vector.tensor_tensor(x[:], clamped[:], gate[:], OP.mult)
+                nc.tensor.matmul(banks[c][:], weights[:, k, :], x[:], start=k == 0, stop=k == BLOCKS - 1)
+
+        for c in range(N // PIECE):
+            result = work.tile([M, PIECE], F32, name="result")
+            nc.scalar.activation(result[:], banks[c][:], FUNC.Relu, bias=bias[:])
+            nc.sync.dma_start(out[:, c * PIECE : (c + 1) * PIECE], result[:])

@@ -10,7 +10,7 @@ S = 2048
 N = 2048
 M = 128
 BLOCKS = R // P
-PIECE = 512
+PIECES = [(0, 512), (512, 512), (1024, 512), (1536, 256), (1792, 256)]
 LOW, HIGH = -1.25, 1.0
 
 FLOPS = 2 * R * M * N
@@ -26,34 +26,33 @@ def tile_lookup_vg_clipsig_relu_kernel(tc, tab, w, b, offs, out):
         offsets = held.tile([P, N // 16], U16, name="offsets")
         nc.sync.dma_start(offsets[:], offs)
 
-        values, gates = [], []
-        for k in range(BLOCKS):
-            rows = slice(k * P, (k + 1) * P)
-            value_window = held.tile([P, S], F32, name=f"value_window{k}")
-            gate_window = held.tile([P, S], F32, name=f"gate_window{k}")
-            nc.sync.dma_start(value_window[:], tab[0, rows, :])
-            nc.sync.dma_start(gate_window[:], tab[1, rows, :])
-            values.append(value_window)
-            gates.append(gate_window)
-
+        gates = [held.tile([P, S], F32, name=f"gate_window{k}") for k in range(BLOCKS)]
+        values = [held.tile([P, S], F32, name=f"value_window{k}") for k in range(BLOCKS)]
         weights = held.tile([P, BLOCKS, M], BF16, name="weights")
-        nc.gpsimd.dma_start(weights[:], w.rearrange("(k p) m -> p k m", p=P))
         bias = held.tile([M, 1], F32, name="bias")
-        nc.gpsimd.dma_start(bias[:], b)
+        nc.sync.dma_start(gates[0][:], tab[1, 0:P, :])
+        nc.sync.dma_start(values[0][:], tab[0, 0:P, :])
+        nc.sync.dma_start(weights[:], w.rearrange("(k p) m -> p k m", p=P))
+        for k in range(1, BLOCKS):
+            nc.sync.dma_start(gates[k][:], tab[1, k * P : (k + 1) * P, :])
+            nc.sync.dma_start(values[k][:], tab[0, k * P : (k + 1) * P, :])
+        nc.sync.dma_start(bias[:], b)
 
-        banks = [sums.tile([M, PIECE], F32, name=f"bank{c}") for c in range(N // PIECE)]
+        banks = [sums.tile([M, width], F32, name=f"bank{c}") for c, (first, width) in enumerate(PIECES)]
         for k in range(BLOCKS):
-            for c in range(N // PIECE):
-                piece = offsets[:, c * PIECE // 16 : (c + 1) * PIECE // 16]
-                clamped = work.tile([P, PIECE], F32, name="clamped")
-                nc.vector.tensor_scalar(clamped[:], values[k][:].indirect(piece), LOW, HIGH, OP.max, OP.min)
-                gate = work.tile([P, PIECE], F32, name="gate")
+            for c, (first, width) in enumerate(PIECES):
+                piece = offsets[:, first // 16 : (first + width) // 16]
+                gate = work.tile([P, width], F32, name="gate")
                 nc.scalar.activation(gate[:], gates[k][:].indirect(piece), FUNC.Sigmoid)
-                x = work.tile([P, PIECE], BF16, name="x")
-                nc.vector.tensor_tensor(x[:], clamped[:], gate[:], OP.mult)
+                clamped = work.tile([P, width], F32, name="clamped")
+                nc.vector.tensor_scalar(clamped[:], values[k][:].indirect(piece), LOW, HIGH, OP.max, OP.min)
+                x = work.tile([P, width], BF16, name="x")
+                last = k == BLOCKS - 1 and c == len(PIECES) - 1
+                multiplier = nc.vector if last else nc.gpsimd
+                multiplier.tensor_tensor(x[:], clamped[:], gate[:], OP.mult)
                 nc.tensor.matmul(banks[c][:], weights[:, k, :], x[:], start=k == 0, stop=k == BLOCKS - 1)
 
-        for c in range(N // PIECE):
-            result = work.tile([M, PIECE], F32, name="result")
+        for c, (first, width) in enumerate(PIECES):
+            result = work.tile([M, width], F32, name="result")
             nc.scalar.activation(result[:], banks[c][:], FUNC.Relu, bias=bias[:])
-            nc.sync.dma_start(out[:, c * PIECE : (c + 1) * PIECE], result[:])
+            nc.sync.dma_start(out[:, first : first + width], result[:])

@@ -23,6 +23,11 @@ def tile_lookup_vg_clipsig_relu_kernel(tc, tab, w, b, offs, out):
         tc.tile_pool(name="work", bufs=4) as work,
         tc.psum_pool(name="sums", bufs=1) as sums,
     ):
+        zeros = held.tile([P, 1], F32, name="zeros")
+        nc.gpsimd.memset(zeros[:], 0.0)
+        warmed = held.tile([P, 1], F32, name="warmed")
+        nc.scalar.activation(warmed[:], zeros[:], FUNC.Sigmoid)
+
         offsets = held.tile([P, N // 16], U16, name="offsets")
         nc.sync.dma_start(offsets[:], offs)
 

import concourse.mybir as mybir

F32, BF16, U16 = mybir.dt.float32, mybir.dt.bfloat16, mybir.dt.uint16
OP = mybir.AluOpType
FUNC = mybir.ActivationFunctionType

P = 128
R = 256
S = 2048
N = 2048
M = 128
BLOCKS = R // P
PIECES = [(0, 512), (512, 512), (1024, 512), (1536, 256), (1792, 256)]
LOW, HIGH = -1.25, 1.0

FLOPS = 2 * R * M * N


def tile_lookup_vg_clipsig_relu_kernel(tc, tab, w, b, offs, out):
    nc = tc.nc
    with (
        tc.tile_pool(name="held", bufs=1) as held,
        tc.tile_pool(name="work", bufs=4) as work,
        tc.psum_pool(name="sums", bufs=1) as sums,
    ):
        zeros = held.tile([P, 1], F32, name="zeros")
        nc.gpsimd.memset(zeros[:], 0.0)
        warmed = held.tile([P, 1], F32, name="warmed")
        nc.scalar.activation(warmed[:], zeros[:], FUNC.Sigmoid)

        offsets = held.tile([P, N // 16], U16, name="offsets")
        nc.sync.dma_start(offsets[:], offs)

        gates = [held.tile([P, S], F32, name=f"gate_window{k}") for k in range(BLOCKS)]
        values = [held.tile([P, S], F32, name=f"value_window{k}") for k in range(BLOCKS)]
        weights = held.tile([P, BLOCKS, M], BF16, name="weights")
        bias = held.tile([M, 1], F32, name="bias")
        nc.sync.dma_start(gates[0][:], tab[1, 0:P, :])
        nc.sync.dma_start(values[0][:], tab[0, 0:P, :])
        nc.sync.dma_start(weights[:], w.rearrange("(k p) m -> p k m", p=P))
        for k in range(1, BLOCKS):
            nc.sync.dma_start(gates[k][:], tab[1, k * P : (k + 1) * P, :])
            nc.sync.dma_start(values[k][:], tab[0, k * P : (k + 1) * P, :])
        nc.sync.dma_start(bias[:], b)

        banks = [sums.tile([M, width], F32, name=f"bank{c}") for c, (first, width) in enumerate(PIECES)]
        for k in range(BLOCKS):
            for c, (first, width) in enumerate(PIECES):
                piece = offsets[:, first // 16 : (first + width) // 16]
                gate = work.tile([P, width], F32, name="gate")
                nc.scalar.activation(gate[:], gates[k][:].indirect(piece), FUNC.Sigmoid)
                clamped = work.tile([P, width], F32, name="clamped")
                nc.vector.tensor_scalar(clamped[:], values[k][:].indirect(piece), LOW, HIGH, OP.max, OP.min)
                x = work.tile([P, width], BF16, name="x")
                last = k == BLOCKS - 1 and c == len(PIECES) - 1
                multiplier = nc.vector if last else nc.gpsimd
                multiplier.tensor_tensor(x[:], clamped[:], gate[:], OP.mult)
                nc.tensor.matmul(banks[c][:], weights[:, k, :], x[:], start=k == 0, stop=k == BLOCKS - 1)

        for c, (first, width) in enumerate(PIECES):
            result = work.tile([M, width], F32, name="result")
            nc.scalar.activation(result[:], banks[c][:], FUNC.Relu, bias=bias[:])
            nc.sync.dma_start(out[:, first : first + width], result[:])
